import numpy as np
import ml_dtypes


def mxq(x, axis, fmt="e4m3"):
    dtype, down = {"e4m3": (ml_dtypes.float8_e4m3fn, 7), "e5m2": (ml_dtypes.float8_e5m2, 14)}[fmt]
    v = np.moveaxis(np.asarray(x, np.float32).astype(ml_dtypes.bfloat16).astype(np.float64), axis, -1)
    blocks = v.reshape(v.shape[:-1] + (-1, 32))
    amax = np.abs(blocks).max(-1, keepdims=True)
    byte = np.maximum(np.where(amax > 0, np.frexp(amax)[1] - 1 + 127, 0) - down, 1)
    scale = np.exp2(byte - 127.0)
    codes = (blocks / scale).astype(np.float32).astype(dtype).astype(np.float64)
    return np.moveaxis((codes * scale).reshape(v.shape), -1, axis)


WIDE = False


def mx_kscale(k):
    if not WIDE:
        return np.ones(k)
    levels = np.array([24, -24, 12, -12, 0])
    if k % 512:
        return np.exp2(np.random.permutation(np.resize(levels, k // 32))).repeat(32)
    a = np.empty((k // 512, 16))
    for p in range(k // 512):
        a[p, :8] = np.random.permutation(np.resize(levels, 8))
        for g in range(8):
            far = levels[np.abs(levels - a[p, g]) >= 10]
            a[p, g + 8] = far[np.random.randint(len(far))]
    return np.exp2(a.ravel()).repeat(32)


def f64(x):
    return np.asarray(x).astype(np.float64)


def striped(idx):
    return np.tile(idx.reshape(-1, 16).T, (8, 1)).astype(np.uint16)


def unstriped(offs):
    return offs[:16].T.reshape(-1).astype(np.int64)


E2M1 = np.array([0.0, 0.5, 1.0, 1.5, 2.0, 3.0, 4.0, 6.0, -0.0, -0.5, -1.0, -1.5, -2.0, -3.0, -4.0, -6.0])


def pack_weight(w, fmt):
    k, n = w.shape
    w = f64(np.asarray(w, np.float32).astype(ml_dtypes.bfloat16)).reshape(k // 32, 32, n)
    amax = np.abs(w).max(1)
    if fmt == "e4m3":
        byte = np.frexp(amax)[1] - 1 + 127 - 7
    else:
        mant, ex = np.frexp(amax / 6.0)
        byte = np.where(mant > 0.5, ex, ex - 1) + 127
    byte = np.clip(np.where(amax > 0, byte, 1), 1, 254)
    scaled = (w * np.exp2(127.0 - byte)[:, None, :]).reshape(k, n).astype(np.float32)
    by_word = np.ascontiguousarray(scaled.reshape(k // 512, 128, 4, n).transpose(0, 1, 3, 2))
    if fmt == "e4m3":
        words = by_word.astype(ml_dtypes.float8_e4m3fn).view(np.uint8)
    else:
        c = by_word.astype(ml_dtypes.float4_e2m1fn).view(np.uint8) & 0xF
        words = (c[..., 0::2] | (c[..., 1::2] << 4)).reshape(k // 512, 128, 2 * n)
    return np.ascontiguousarray(words), np.ascontiguousarray(byte.astype(np.uint8).reshape(k // 512, 16, n))


def unpack_weight(words, scales, fmt):
    g, _, n = scales.shape
    words = np.ascontiguousarray(words).reshape(g, 128, n, -1)
    if fmt == "e4m3":
        vals = words.view(ml_dtypes.float8_e4m3fn).astype(np.float64)
    else:
        nib = np.empty((g, 128, n, 4), np.uint8)
        nib[..., 0::2] = words & 0xF
        nib[..., 1::2] = words >> 4
        vals = E2M1[nib]
    vals = vals * np.repeat(np.exp2(scales.astype(np.float64) - 127.0), 8, axis=1)[..., None]
    return vals.transpose(0, 1, 3, 2).reshape(g * 512, n)


def pack_table4(v):
    words, scales = pack_weight(v, "e2m1")
    g, t = words.shape[0] // 2, v.shape[1]
    return np.ascontiguousarray(words.reshape(g, 2, 128, t, 2).transpose(0, 2, 3, 1, 4).reshape(g, 128, t, 4)), scales


def unpack_table4(words, scales):
    g, _, t, _ = words.shape
    return unpack_weight(words.reshape(g, 128, t, 2, 2).transpose(0, 3, 1, 2, 4).reshape(2 * g, 128, 2 * t), scales, "e2m1")


def sigm(f):
    return 1.0 / (1.0 + np.exp(-np.maximum(f, -700.0)))


K, R, M, N, T, J = 1024, 1024, 512, 256, 4096, 1024


def setup_inputs():
    n = np.random.standard_normal
    s = mx_kscale(K)[:, None]
    s2 = mx_kscale(K)[:, None]
    u = mx_kscale(R)[:, None]
    p_tab = pack_table4(n((K, T)) * s2)
    p_wq = pack_weight(n((K, R)) / np.sqrt(K) / s / u.T, "e2m1")
    p_wv4 = pack_weight(n((K, N)) / np.sqrt(K) / s2, "e2m1")
    return {
        "tab_words": p_tab[0],
        "tab_scales": p_tab[1],
        "x": (n((K, M)) * s).astype(np.float32),
        "wq_words": p_wq[0],
        "wq_scales": p_wq[1],
        "wk": (n((K, R)) / np.sqrt(K) / s2 * u.T).astype(np.float32),
        "wv4_words": p_wv4[0],
        "wv4_scales": p_wv4[1],
        "wvd": (0.4 * (n((K, N)) / np.sqrt(K) / s2)).astype(np.float32),
        "offs": striped(np.random.permutation(T)[:J]),
    }


def reference(tab_words, tab_scales, x, wq_words, wq_scales, wk, wv4_words, wv4_scales, wvd, offs):
    idx = unstriped(offs)
    tab_ = unpack_table4(tab_words, tab_scales)[:, idx]
    x_ = mxq(f64(x), 0, "e4m3")
    wq_ = unpack_weight(wq_words, wq_scales, "e2m1")
    wk_ = mxq(f64(wk), 0, "e4m3")
    qr = wq_.T @ x_
    kr = wk_.T @ tab_
    qr_ = mxq(qr, 0, "e4m3")
    kr_ = mxq(kr, 0, "e4m3")
    sc = qr_.T @ kr_
    wv4_ = unpack_weight(wv4_words, wv4_scales, "e2m1")
    wvd_ = mxq(f64(wvd), 0, "e4m3")
    vv = wv4_.T @ tab_ + wvd_.T @ tab_
    return sigm(sc * 0.03125), vv

@@ -1,0 +1,255 @@
+from contextlib import ExitStack
+
+import concourse.mybir as mybir
+
+K, R, M, N, T, J = 1024, 1024, 512, 256, 4096, 1024
+FLOPS = 2 * (K * R * M + K * R * J + R * M * J + 2 * K * N * J)
+
+F32 = mybir.dt.float32
+BF16 = mybir.dt.bfloat16
+I32 = mybir.dt.int32
+U32 = mybir.dt.uint32
+U16 = mybir.dt.uint16
+U8 = mybir.dt.uint8
+FP8X4 = mybir.dt.float8_e4m3fn_x4
+FP4X4 = mybir.dt.float4_e2m1fn_x4
+SIGMOID = mybir.ActivationFunctionType.Sigmoid
+
+P = 128
+PACK = 4
+PASS = P * PACK
+BANK = 512
+QUADS = 4
+SCORE_SCALE = 0.03125
+X_VECTOR_GROUPS = 80
+ROWS = 32
+TAB_AT, WQ_AT, WV4_AT, PLANE = 0, J, J + R, J + R + N
+
+
+def tile_list_kvt_dl_sig_kernel(
+    tc, tab_words, tab_scales, x, wq_words, wq_scales, wk, wv4_words, wv4_scales, wvd, offs, out_0, out_1
+):
+    nc = tc.nc
+    k_passes = K // PASS
+    r_passes = R // PASS
+    j_halves = J // BANK
+
+    with ExitStack() as ctx:
+        keep = ctx.enter_context(tc.tile_pool(name="keep", bufs=1))
+        ring = ctx.enter_context(tc.tile_pool(name="ring", bufs=4))
+        psum = ctx.enter_context(tc.psum_pool(name="psum", bufs=8))
+
+        def kept(shape, dtype, name, tag=None):
+            return keep.tile(shape, dtype, name=name, tag=tag or name, align_bytes=64)
+
+        offsets = keep.tile([P, J // 16], U16, name="offsets")
+        nc.sync.dma_start(offsets[:], offs)
+
+        def compact_rows(scales):
+            return scales.rearrange("a q n -> q a n").bitcast(I32)
+
+        scale_rows = kept([P, T], U8, "scale_rows")
+        nc.sync.dma_start(scale_rows[0:ROWS, :].bitcast(I32), compact_rows(tab_scales))
+        compact = kept([ROWS, PLANE], U8, "compact", tag="late")
+        nc.sync.dma_start(compact[:, WV4_AT : WV4_AT + N].bitcast(I32), compact_rows(wv4_scales))
+        wq_rows = kept([ROWS, R], U8, "wq_rows")
+        nc.sync.dma_start(wq_rows[:].bitcast(I32), compact_rows(wq_scales))
+        wv4_codes = kept([P, k_passes, 2 * N], U8, "wv4_codes")
+        nc.sync.dma_start(wv4_codes[:].bitcast(I32), wv4_words.rearrange("a p n -> p a n").bitcast(I32))
+        wq_loaded = kept([P, k_passes * R // 2], I32, "wq_loaded")
+        nc.sync.dma_start(
+            wq_loaded[:].rearrange("p (a n) -> p a n", a=k_passes), wq_words.rearrange("a p n -> p a n").bitcast(I32)
+        )
+        x_raw = [kept([P, PACK * M], F32, f"x_raw{a}") for a in range(k_passes)]
+        for a in range(k_passes):
+            nc.sync.dma_start(x_raw[a][:], x[a * PASS : (a + 1) * PASS, :].rearrange("(p j) m -> p (j m)", j=PACK))
+
+        nc.vector.memset(scale_rows[32:64, :].bitcast(I32), 0)
+        nc.vector.memset(scale_rows[64:128, :].bitcast(I32), 0)
+        planes = kept([P, k_passes * PLANE], U8, "planes")
+        nc.vector.memset(planes[:].bitcast(I32), 0)
+
+        warm_in = kept([P, 1], F32, "warm_in")
+        warm_out = kept([P, 1], F32, "warm_out")
+        nc.gpsimd.memset(warm_in[:], 0.0)
+        nc.scalar.activation(warm_out[:], warm_in[:], SIGMOID, scale=SCORE_SCALE)
+
+        picked_rows = kept([P, J], U8, "picked_rows", tag="table")
+        nc.vector.tensor_copy(picked_rows[:], scale_rows[:].indirect(offsets[:]))
+        nc.vector.tensor_copy(
+            compact[:, WQ_AT : WQ_AT + R].bitcast(I32).rearrange("p (b t h) -> p b t h", t=PACK, h=32),
+            wq_rows[:].bitcast(I32).rearrange("p (b h t) -> p b t h", t=PACK, h=32),
+        )
+        nc.vector.tensor_copy(compact[:, TAB_AT : TAB_AT + J].bitcast(I32), picked_rows[0:ROWS, :].bitcast(I32))
+        for q in (0, 2, 1, 3):
+            nc.sync.dma_start(
+                planes[32 * q : 32 * q + 4, :].bitcast(I32).rearrange("p (a n) -> p a n", a=k_passes),
+                compact[8 * q : 8 * q + 8, :].bitcast(I32),
+            )
+
+        def plane_cols(a, start, cols):
+            first = a * PLANE + start
+            return planes[:, first + cols.start : first + cols.stop]
+
+        table = kept([P, T], I32, "table")
+        nc.sync.dma_start(table[:], tab_words[0].rearrange("p t b -> p (t b)").bitcast(I32))
+
+        raw = kept([P, (1 + k_passes * r_passes) * PACK * BANK], F32, "raw", tag="late")
+
+        def raw_chunk(i):
+            return raw[:, i * PACK * BANK : (i + 1) * PACK * BANK]
+
+        wvd_raw = raw_chunk(0)
+        for a in range(k_passes):
+            nc.sync.dma_start(
+                wvd_raw[:, a * PACK * N : (a + 1) * PACK * N],
+                wvd[a * PASS : (a + 1) * PASS, :].rearrange("(p j) n -> p (j n)", j=PACK),
+            )
+        for b in range(r_passes):
+            for a in range(k_passes):
+                nc.sync.dma_start(
+                    raw_chunk(1 + k_passes * b + a).rearrange("p (j r) -> p j r", j=PACK),
+                    wk[a * PASS : (a + 1) * PASS, b * PASS : (b + 1) * PASS].rearrange("(p j) r -> p j r", j=PACK),
+                )
+
+        def tab_operand(a, h, cols):
+            codes = tab_codes[h][:, a, 2 * cols.start : 2 * cols.stop].bitcast(FP4X4)
+            return codes, plane_cols(a, TAB_AT + h * BANK, cols)
+
+        def quantize(rounded, width, name):
+            codes = kept([P, width], U32, name + "_codes")
+            plane = kept([P, width], U8, name + "_plane")
+            nc.vector.quantize_mx(out=codes[:].bitcast(FP8X4), scales=plane[:], in_=rounded)
+            return codes, plane
+
+        def fp8_operand(quantized, cols):
+            codes, plane = quantized
+            return codes[:, cols].bitcast(FP8X4), plane[:, cols]
+
+        def mx(out, stationary, moving, start, stop):
+            nc.tensor.matmul_mx(
+                out=out, lhsT=stationary[0], lhsT_scale=stationary[1], rhs=moving[0], rhs_scale=moving[1],
+                start=start, stop=stop,
+            )
+
+        def tile_cols(i, width=P):
+            return slice(i * width, (i + 1) * width)
+
+        wq_codes = kept([P, k_passes * 2 * R], U8, "wq_codes")
+        nc.vector.tensor_copy(
+            wq_codes[:].bitcast(I32).rearrange("p (g t h w) -> p g t h w", t=PACK, h=32, w=2),
+            wq_loaded[:].rearrange("p (g h t w) -> p g t h w", t=PACK, h=32, w=2),
+        )
+
+        x_q = []
+        for a in range(k_passes):
+            rounded = ring.tile([P, PACK * BANK], BF16, name="rounded", align_bytes=64)
+            dst = rounded[:].rearrange("p (c i j) -> p c j i", i=4, j=PACK)
+            src = x_raw[a][:].rearrange("p (j c i) -> p c j i", i=4, j=PACK)
+            nc.vector.tensor_copy(dst[:, :X_VECTOR_GROUPS], src[:, :X_VECTOR_GROUPS])
+            nc.scalar.copy(dst[:, X_VECTOR_GROUPS:], src[:, X_VECTOR_GROUPS:])
+            x_q.append(quantize(rounded[:], M, f"x{a}"))
+
+        def project(waves, copies):
+            banks = [[psum.tile([P, BANK], F32, name="bank") for c in range(BANK // P)] for wave in waves]
+            rounded = [ring.tile([P, PACK * BANK], BF16, name="projected", align_bytes=64) for wave in waves]
+            for a in range(k_passes):
+                for w, (stationary, moving) in enumerate(waves):
+                    for c, bank in enumerate(banks[w]):
+                        for t in range(PACK):
+                            first = a == 0 and t == 0
+                            last = a == k_passes - 1 and t == PACK - 1
+                            mx(bank[:, tile_cols(t)], stationary(a, t), moving(a, tile_cols(c)), first, last)
+                        if a == k_passes - 1:
+                            copies[c % len(copies)](
+                                rounded[w][:, tile_cols(c, BANK)].rearrange("p (n t) -> p n t", t=PACK),
+                                bank[:].rearrange("p (t n) -> p n t", t=PACK),
+                            )
+            return rounded
+
+        def wq_operand(b):
+            def operand(a, t):
+                col = PACK * b + t
+                codes = wq_codes[:, tile_cols(PACK * r_passes * a + col, 2 * P)].bitcast(FP4X4)
+                return codes, plane_cols(a, WQ_AT, tile_cols(col))
+
+            return operand
+
+        q_rounded = []
+        for b in range(r_passes):
+            wave = (wq_operand(b), lambda a, cols: fp8_operand(x_q[a], cols))
+            q_rounded.extend(project([wave], [nc.vector.tensor_copy, nc.scalar.copy] if b == 0 else [nc.scalar.copy]))
+
+        tab_codes = []
+        for h in range(j_halves):
+            picked = kept([P, BANK], U32, f"picked{h}", tag="picked")
+            nc.vector.tensor_copy(picked[:], table[:].bitcast(U32).indirect(offsets[:, 32 * h : 32 * (h + 1)]))
+            parted = kept([P, k_passes, 2 * BANK], U8, f"tab_codes{h}")
+            nc.vector.tensor_copy(
+                parted[:].bitcast(U16), picked[:].bitcast(U16).rearrange("p (j d) -> p d j", d=k_passes)
+            )
+            tab_codes.append(parted)
+
+        wvd_q = []
+        for a in range(k_passes):
+            rounded = ring.tile([P, PACK * N], BF16, name="wvd_rounded", align_bytes=64)
+            nc.scalar.copy(
+                rounded[:].rearrange("p (c i j) -> p c j i", i=4, j=PACK),
+                wvd_raw[:, tile_cols(a, PACK * N)].rearrange("p (j c i) -> p c j i", i=4, j=PACK),
+            )
+            wvd_q.append(quantize(rounded[:], N, f"wvd{a}"))
+
+        whole = slice(0, BANK)
+        v_banks = {}
+        for h in range(j_halves):
+            for n in range(N // P):
+                v_banks[h, n] = psum.tile([P, BANK], F32, name="bank")
+                for a in range(k_passes):
+                    base = (
+                        wv4_codes[:, a, tile_cols(n, 2 * P)].bitcast(FP4X4),
+                        plane_cols(a, WV4_AT, tile_cols(n)),
+                    )
+                    mx(v_banks[h, n][:], base, tab_operand(a, h, whole), a == 0, False)
+        values = [kept([P, J], F32, f"values{n}") for n in range(N // P)]
+        for a in range(k_passes):
+            for n in range(N // P):
+                for h in range(j_halves):
+                    last = a == k_passes - 1
+                    mx(v_banks[h, n][:], fp8_operand(wvd_q[a], tile_cols(n)), tab_operand(a, h, whole), False, last)
+                    if last:
+                        nc.scalar.copy(values[n][:, tile_cols(h, BANK)], v_banks[h, n][:])
+
+        wk_q = {}
+        for b in range(r_passes):
+            for a in range(k_passes):
+                rounded = ring.tile([P, PACK * BANK], BF16, name="rounded", align_bytes=64)
+                dst = rounded[:].rearrange("p (t h i j) -> p t h j i", t=PACK, i=4, j=PACK)
+                src = raw_chunk(1 + k_passes * b + a).rearrange("p (j h t i) -> p t h j i", t=PACK, i=4, j=PACK)
+                if a == 0 and b == 0:
+                    nc.vector.tensor_copy(dst[:, :2], src[:, :2])
+                    nc.scalar.copy(dst[:, 2:], src[:, 2:])
+                else:
+                    nc.vector.tensor_copy(dst, src)
+                wk_q[a, b] = quantize(rounded[:], PASS, f"wk{b}{a}")
+
+        q_q = [quantize(q_rounded[b][:], BANK, f"qr{b}") for b in range(r_passes)]
+
+        k_q = {}
+        for b in range(r_passes):
+            for h in range(j_halves):
+                final = b == r_passes - 1 and h == j_halves - 1
+                wave = (lambda a, t: fp8_operand(wk_q[a, b], tile_cols(t)), lambda a, cols: tab_operand(a, h, cols))
+                k_rounded = project([wave], [nc.vector.tensor_copy] if final else [nc.scalar.copy])
+                k_q[b, h] = quantize(k_rounded[0][:], BANK, f"kr{b}{h}")
+
+        for n in range(N // P):
+            nc.sync.dma_start(out_1[tile_cols(n), :], values[n][:])
+
+        for h in range(j_halves):
+            for m in range(M // P):
+                bank = psum.tile([P, BANK], F32, name="bank")
+                for b in range(r_passes):
+                    mx(bank[:], fp8_operand(q_q[b], tile_cols(m)), fp8_operand(k_q[b, h], whole), b == 0, b == r_passes - 1)
+                gates = kept([P, BANK], F32, f"gates{h}{m}")
+                nc.scalar.activation(gates[:], bank[:], SIGMOID, scale=SCORE_SCALE)
+                nc.sync.dma_start(out_0[tile_cols(m), tile_cols(h, BANK)], gates[:])

@@ -21,9 +21,9 @@ PASS = P * PACK
 BANK = 512
 QUADS = 4
 SCORE_SCALE = 0.03125
-X_VECTOR_GROUPS = 80
 ROWS = 32
-TAB_AT, WQ_AT, WV4_AT, PLANE = 0, J, J + R, J + R + N
+TAB_AT, WV4_AT, PLANE = 0, J, J + N
+LATE_BYTES = 4 * 13312
 
 
 def tile_list_kvt_dl_sig_kernel(
@@ -36,7 +36,8 @@ def tile_list_kvt_dl_sig_kernel(
 
     with ExitStack() as ctx:
         keep = ctx.enter_context(tc.tile_pool(name="keep", bufs=1))
-        ring = ctx.enter_context(tc.tile_pool(name="ring", bufs=4))
+        ring = ctx.enter_context(tc.tile_pool(name="ring", bufs=2))
+        staged = ctx.enter_context(tc.tile_pool(name="staged", bufs=1))
         psum = ctx.enter_context(tc.psum_pool(name="psum", bufs=8))
 
         def kept(shape, dtype, name, tag=None):
@@ -50,77 +51,84 @@ def tile_list_kvt_dl_sig_kernel(
 
         scale_rows = kept([P, T], U8, "scale_rows")
         nc.sync.dma_start(scale_rows[0:ROWS, :].bitcast(I32), compact_rows(tab_scales))
-        compact = kept([ROWS, PLANE], U8, "compact", tag="late")
+        compact = kept([ROWS, PLANE], U8, "compact")
         nc.sync.dma_start(compact[:, WV4_AT : WV4_AT + N].bitcast(I32), compact_rows(wv4_scales))
         wq_rows = kept([ROWS, R], U8, "wq_rows")
         nc.sync.dma_start(wq_rows[:].bitcast(I32), compact_rows(wq_scales))
+        table = kept([P, T], I32, "table")
+        nc.sync.dma_start(table[:], tab_words[0].rearrange("p t b -> p (t b)").bitcast(I32))
+
         wv4_codes = kept([P, k_passes, 2 * N], U8, "wv4_codes")
         nc.sync.dma_start(wv4_codes[:].bitcast(I32), wv4_words.rearrange("a p n -> p a n").bitcast(I32))
-        wq_loaded = kept([P, k_passes * R // 2], I32, "wq_loaded")
-        nc.sync.dma_start(
-            wq_loaded[:].rearrange("p (a n) -> p a n", a=k_passes), wq_words.rearrange("a p n -> p a n").bitcast(I32)
-        )
-        x_raw = [kept([P, PACK * M], F32, f"x_raw{a}") for a in range(k_passes)]
-        for a in range(k_passes):
-            nc.sync.dma_start(x_raw[a][:], x[a * PASS : (a + 1) * PASS, :].rearrange("(p j) m -> p (j m)", j=PACK))
-
+        wvd_raw0 = kept([P, 1024], F32, "wvd_raw0")[:]
+        nc.sync.dma_start(wvd_raw0, wvd[0 * PASS : 1 * PASS, :].rearrange("(p j) n -> p (j n)", j=PACK))
         nc.vector.memset(scale_rows[32:64, :].bitcast(I32), 0)
         nc.vector.memset(scale_rows[64:128, :].bitcast(I32), 0)
         planes = kept([P, k_passes * PLANE], U8, "planes")
         nc.vector.memset(planes[:].bitcast(I32), 0)
+        wq_planes = kept([P, k_passes * R], U8, "wq_planes")
+        nc.vector.memset(wq_planes[:].bitcast(I32), 0)
 
         warm_in = kept([P, 1], F32, "warm_in")
         warm_out = kept([P, 1], F32, "warm_out")
         nc.gpsimd.memset(warm_in[:], 0.0)
         nc.scalar.activation(warm_out[:], warm_in[:], SIGMOID, scale=SCORE_SCALE)
 
-        picked_rows = kept([P, J], U8, "picked_rows", tag="table")
+        def place(target, rows):
+            for q in (0, 2, 1, 3):
+                nc.sync.dma_start(
+                    target[32 * q : 32 * q + 4, :].bitcast(I32).rearrange("p (a n) -> p a n", a=k_passes),
+                    rows[8 * q : 8 * q + 8, :].bitcast(I32),
+                )
+
+        picked_rows = staged.tile([P, J], U8, name="picked_rows", align_bytes=64, offset=LATE_BYTES - J // 2)
         nc.vector.tensor_copy(picked_rows[:], scale_rows[:].indirect(offsets[:]))
+        nc.vector.tensor_copy(compact[:, TAB_AT : TAB_AT + J].bitcast(I32), picked_rows[0:ROWS, :].bitcast(I32))
+        place(planes, compact)
+        wq_compact = staged.tile([ROWS, R], U8, name="wq_compact", align_bytes=64, offset=LATE_BYTES)
         nc.vector.tensor_copy(
-            compact[:, WQ_AT : WQ_AT + R].bitcast(I32).rearrange("p (b t h) -> p b t h", t=PACK, h=32),
+            wq_compact[:].bitcast(I32).rearrange("p (b t h) -> p b t h", t=PACK, h=32),
             wq_rows[:].bitcast(I32).rearrange("p (b h t) -> p b t h", t=PACK, h=32),
         )
-        nc.vector.tensor_copy(compact[:, TAB_AT : TAB_AT + J].bitcast(I32), picked_rows[0:ROWS, :].bitcast(I32))
-        for q in (0, 2, 1, 3):
-            nc.sync.dma_start(
-                planes[32 * q : 32 * q + 4, :].bitcast(I32).rearrange("p (a n) -> p a n", a=k_passes),
-                compact[8 * q : 8 * q + 8, :].bitcast(I32),
-            )
 
         def plane_cols(a, start, cols):
             first = a * PLANE + start
             return planes[:, first + cols.start : first + cols.stop]
 
-        table = kept([P, T], I32, "table")
-        nc.sync.dma_start(table[:], tab_words[0].rearrange("p t b -> p (t b)").bitcast(I32))
-
-        raw = kept([P, (1 + k_passes * r_passes) * PACK * BANK], F32, "raw", tag="late")
-
-        def raw_chunk(i):
-            return raw[:, i * PACK * BANK : (i + 1) * PACK * BANK]
-
-        wvd_raw = raw_chunk(0)
-        for a in range(k_passes):
-            nc.sync.dma_start(
-                wvd_raw[:, a * PACK * N : (a + 1) * PACK * N],
-                wvd[a * PASS : (a + 1) * PASS, :].rearrange("(p j) n -> p (j n)", j=PACK),
-            )
-        for b in range(r_passes):
-            for a in range(k_passes):
-                nc.sync.dma_start(
-                    raw_chunk(1 + k_passes * b + a).rearrange("p (j r) -> p j r", j=PACK),
-                    wk[a * PASS : (a + 1) * PASS, b * PASS : (b + 1) * PASS].rearrange("(p j) r -> p j r", j=PACK),
-                )
+        late = staged.tile([P, 13312], F32, name="late", align_bytes=64, offset=0)
+        wvd_raw1 = late[:, 0 : 1024]
+        nc.sync.dma_start(wvd_raw1, wvd[1 * PASS : 2 * PASS, :].rearrange("(p j) n -> p (j n)", j=PACK))
+        wk_raw00 = late[:, 5120 : 7168]
+        nc.sync.dma_start(wk_raw00.rearrange("p (j r) -> p j r", j=PACK), wk[0 * PASS : 1 * PASS, 0 * PASS : 1 * PASS].rearrange("(p j) r -> p j r", j=PACK))
+        wk_raw01 = late[:, 7168 : 9216]
+        nc.sync.dma_start(wk_raw01.rearrange("p (j r) -> p j r", j=PACK), wk[1 * PASS : 2 * PASS, 0 * PASS : 1 * PASS].rearrange("(p j) r -> p j r", j=PACK))
+        x_raw0 = late[:, 1024 : 3072]
+        nc.sync.dma_start(x_raw0, x[0 * PASS : 1 * PASS, :].rearrange("(p j) m -> p (j m)", j=PACK))
+        wq_loaded = kept([P, k_passes * R // 2], I32, "wq_loaded", tag="wq_rows")
+        nc.sync.dma_start(
+            wq_loaded[:].rearrange("p (a n) -> p a n", a=k_passes), wq_words.rearrange("a p n -> p a n").bitcast(I32)
+        )
+        place(wq_planes, wq_compact)
+        x_raw1 = late[:, 3072 : 5120]
+        nc.sync.dma_start(x_raw1, x[1 * PASS : 2 * PASS, :].rearrange("(p j) m -> p (j m)", j=PACK))
+        wk_raw10 = late[:, 9216 : 11264]
+        nc.sync.dma_start(wk_raw10.rearrange("p (j r) -> p j r", j=PACK), wk[0 * PASS : 1 * PASS, 1 * PASS : 2 * PASS].rearrange("(p j) r -> p j r", j=PACK))
+        wk_raw11 = late[:, 11264 : 13312]
+        nc.sync.dma_start(wk_raw11.rearrange("p (j r) -> p j r", j=PACK), wk[1 * PASS : 2 * PASS, 1 * PASS : 2 * PASS].rearrange("(p j) r -> p j r", j=PACK))
+        x_raw = [x_raw0, x_raw1]
+        wvd_raw = [wvd_raw0, wvd_raw1]
+        wk_raw = {(0, 0): wk_raw00, (0, 1): wk_raw01, (1, 0): wk_raw10, (1, 1): wk_raw11}
 
         def tab_operand(a, h, cols):
             codes = tab_codes[h][:, a, 2 * cols.start : 2 * cols.stop].bitcast(FP4X4)
             return codes, plane_cols(a, TAB_AT + h * BANK, cols)
 
-        def quantize(rounded, width, name):
-            codes = kept([P, width], U32, name + "_codes")
-            plane = kept([P, width], U8, name + "_plane")
-            nc.vector.quantize_mx(out=codes[:].bitcast(FP8X4), scales=plane[:], in_=rounded)
-            return codes, plane
+        def mx_tiles(width, name, tag=None):
+            return kept([P, width], U32, name + "_codes", tag=tag), kept([P, width], U8, name + "_plane")
+
+        def quantize(quantized, cols, rounded):
+            codes, plane = quantized
+            nc.vector.quantize_mx(out=codes[:, cols].bitcast(FP8X4), scales=plane[:, cols], in_=rounded)
 
         def fp8_operand(quantized, cols):
             codes, plane = quantized
@@ -135,24 +143,9 @@ def tile_list_kvt_dl_sig_kernel(
         def tile_cols(i, width=P):
             return slice(i * width, (i + 1) * width)
 
-        wq_codes = kept([P, k_passes * 2 * R], U8, "wq_codes")
-        nc.vector.tensor_copy(
-            wq_codes[:].bitcast(I32).rearrange("p (g t h w) -> p g t h w", t=PACK, h=32, w=2),
-            wq_loaded[:].rearrange("p (g h t w) -> p g t h w", t=PACK, h=32, w=2),
-        )
-
-        x_q = []
-        for a in range(k_passes):
-            rounded = ring.tile([P, PACK * BANK], BF16, name="rounded", align_bytes=64)
-            dst = rounded[:].rearrange("p (c i j) -> p c j i", i=4, j=PACK)
-            src = x_raw[a][:].rearrange("p (j c i) -> p c j i", i=4, j=PACK)
-            nc.vector.tensor_copy(dst[:, :X_VECTOR_GROUPS], src[:, :X_VECTOR_GROUPS])
-            nc.scalar.copy(dst[:, X_VECTOR_GROUPS:], src[:, X_VECTOR_GROUPS:])
-            x_q.append(quantize(rounded[:], M, f"x{a}"))
-
         def project(waves, copies):
             banks = [[psum.tile([P, BANK], F32, name="bank") for c in range(BANK // P)] for wave in waves]
-            rounded = [ring.tile([P, PACK * BANK], BF16, name="projected", align_bytes=64) for wave in waves]
+            rounded = [ring.tile([P, PACK * BANK], BF16, name="projected", bufs=6, align_bytes=64) for wave in waves]
             for a in range(k_passes):
                 for w, (stationary, moving) in enumerate(waves):
                     for c, bank in enumerate(banks[w]):
@@ -171,14 +164,9 @@ def tile_list_kvt_dl_sig_kernel(
             def operand(a, t):
                 col = PACK * b + t
                 codes = wq_codes[:, tile_cols(PACK * r_passes * a + col, 2 * P)].bitcast(FP4X4)
-                return codes, plane_cols(a, WQ_AT, tile_cols(col))
+                return codes, wq_planes[:, tile_cols(PACK * r_passes * a + col)]
 
             return operand
-
-        q_rounded = []
-        for b in range(r_passes):
-            wave = (wq_operand(b), lambda a, cols: fp8_operand(x_q[a], cols))
-            q_rounded.extend(project([wave], [nc.vector.tensor_copy, nc.scalar.copy] if b == 0 else [nc.scalar.copy]))
 
         tab_codes = []
         for h in range(j_halves):
@@ -193,12 +181,32 @@ def tile_list_kvt_dl_sig_kernel(
         wvd_q = []
         for a in range(k_passes):
             rounded = ring.tile([P, PACK * N], BF16, name="wvd_rounded", align_bytes=64)
-            nc.scalar.copy(
+            [nc.scalar.copy, nc.scalar.copy][a](
                 rounded[:].rearrange("p (c i j) -> p c j i", i=4, j=PACK),
-                wvd_raw[:, tile_cols(a, PACK * N)].rearrange("p (j c i) -> p c j i", i=4, j=PACK),
+                wvd_raw[a].rearrange("p (j c i) -> p c j i", i=4, j=PACK),
             )
-            wvd_q.append(quantize(rounded[:], N, f"wvd{a}"))
+            wvd_q.append(mx_tiles(N, f"wvd{a}"))
+            quantize(wvd_q[a], slice(0, N), rounded[:])
 
+        wk_q = {}
+
+        def prepare_wk(b):
+            for a in range(k_passes):
+                rounded = kept([P, PACK * BANK], BF16, f"wk_rounded{b}{a}")
+                dst = rounded[:].rearrange("p (t h i j) -> p t h j i", t=PACK, i=4, j=PACK)
+                src = wk_raw[b, a].rearrange("p (j h t i) -> p t h j i", t=PACK, i=4, j=PACK)
+                wk_q[a, b] = mx_tiles(PASS, f"wk{b}{a}")
+                for half in range(2):
+                    copy = [nc.vector.tensor_copy, nc.scalar.copy, nc.vector.tensor_copy, nc.vector.tensor_copy, nc.vector.tensor_copy, nc.vector.tensor_copy, nc.vector.tensor_copy, nc.vector.tensor_copy][4 * b + 2 * a + half]
+                    copy(dst[:, tile_cols(half, 2)], src[:, tile_cols(half, 2)])
+                for half in range(2):
+                    quantize(wk_q[a, b], tile_cols(half, PASS // 2), rounded[:, tile_cols(half, PACK * PASS // 2)])
+
+        def keys(b, h):
+            wave = (lambda a, t: fp8_operand(wk_q[a, b], tile_cols(t)), lambda a, cols: tab_operand(a, h, cols))
+            return project([wave], [[nc.scalar.copy], [nc.scalar.copy], [nc.scalar.copy, nc.scalar.copy, nc.scalar.copy, nc.vector.tensor_copy], [nc.scalar.copy, nc.vector.tensor_copy]][2 * b + h])[0]
+
+        prepare_wk(0)
         whole = slice(0, BANK)
         v_banks = {}
         for h in range(j_halves):
@@ -217,30 +225,43 @@ def tile_list_kvt_dl_sig_kernel(
                     last = a == k_passes - 1
                     mx(v_banks[h, n][:], fp8_operand(wvd_q[a], tile_cols(n)), tab_operand(a, h, whole), False, last)
                     if last:
-                        nc.scalar.copy(values[n][:, tile_cols(h, BANK)], v_banks[h, n][:])
+                        [nc.scalar.copy, nc.scalar.copy, nc.scalar.copy, nc.scalar.copy][2 * n + h](values[n][:, tile_cols(h, BANK)], v_banks[h, n][:])
 
-        wk_q = {}
+        x_q = []
+        for a in range(k_passes):
+            rounded = kept([P, PACK * BANK], BF16, f"x_rounded{a}")
+            dst = rounded[:].rearrange("p (c i j) -> p c j i", i=4, j=PACK)
+            src = x_raw[a].rearrange("p (j c i) -> p c j i", i=4, j=PACK)
+            x_q.append(mx_tiles(M, f"x{a}"))
+            for half, copy in enumerate([[nc.vector.tensor_copy, nc.vector.tensor_copy], [nc.vector.tensor_copy, nc.vector.tensor_copy]][a]):
+                copy(dst[:, tile_cols(half, M // 8)], src[:, tile_cols(half, M // 8)])
+            for half in range(2):
+                quantize(x_q[a], tile_cols(half, M // 2), rounded[:, tile_cols(half, PACK * M // 2)])
+
+        wq_codes = kept([P, k_passes * 2 * R], U8, "wq_codes")
+        nc.vector.tensor_copy(
+            wq_codes[:].bitcast(I32).rearrange("p (g t h w) -> p g t h w", t=PACK, h=32, w=2),
+            wq_loaded[:].rearrange("p (g h t w) -> p g t h w", t=PACK, h=32, w=2),
+        )
+
+        k_rounded = [keys(0, h) for h in range(j_halves)]
+        q_rounded = []
         for b in range(r_passes):
-            for a in range(k_passes):
-                rounded = ring.tile([P, PACK * BANK], BF16, name="rounded", align_bytes=64)
-                dst = rounded[:].rearrange("p (t h i j) -> p t h j i", t=PACK, i=4, j=PACK)
-                src = raw_chunk(1 + k_passes * b + a).rearrange("p (j h t i) -> p t h j i", t=PACK, i=4, j=PACK)
-                if a == 0 and b == 0:
-                    nc.vector.tensor_copy(dst[:, :2], src[:, :2])
-                    nc.scalar.copy(dst[:, 2:], src[:, 2:])
-                else:
-                    nc.vector.tensor_copy(dst, src)
-                wk_q[a, b] = quantize(rounded[:], PASS, f"wk{b}{a}")
+            wave = (wq_operand(b), lambda a, cols: fp8_operand(x_q[a], cols))
+            q_rounded.extend(project([wave], [[nc.scalar.copy], [nc.scalar.copy]][b]))
 
-        q_q = [quantize(q_rounded[b][:], BANK, f"qr{b}") for b in range(r_passes)]
-
-        k_q = {}
+        prepare_wk(1)
+        k_q = [mx_tiles(J, "kr0", tag="x_rounded0"), mx_tiles(J, "kr1")]
+        for h in range(j_halves):
+            quantize(k_q[0], tile_cols(h, BANK), k_rounded[h][:])
+        q_q = mx_tiles(r_passes * M, "qr", tag="wk_rounded11")
         for b in range(r_passes):
-            for h in range(j_halves):
-                final = b == r_passes - 1 and h == j_halves - 1
-                wave = (lambda a, t: fp8_operand(wk_q[a, b], tile_cols(t)), lambda a, cols: tab_operand(a, h, cols))
-                k_rounded = project([wave], [nc.vector.tensor_copy] if final else [nc.scalar.copy])
-                k_q[b, h] = quantize(k_rounded[0][:], BANK, f"kr{b}{h}")
+            quantize(q_q, tile_cols(b, M), q_rounded[b][:])
+
+        for h in range(j_halves):
+            rounded = keys(1, h)
+            for part in range(2):
+                quantize(k_q[1], tile_cols(2 * h + part, BANK // 2), rounded[:, tile_cols(part, PACK * BANK // 2)])
 
         for n in range(N // P):
             nc.sync.dma_start(out_1[tile_cols(n), :], values[n][:])
@@ -249,7 +270,8 @@ def tile_list_kvt_dl_sig_kernel(
             for m in range(M // P):
                 bank = psum.tile([P, BANK], F32, name="bank")
                 for b in range(r_passes):
-                    mx(bank[:], fp8_operand(q_q[b], tile_cols(m)), fp8_operand(k_q[b, h], whole), b == 0, b == r_passes - 1)
+                    queries = fp8_operand(q_q, tile_cols(b * (M // P) + m))
+                    mx(bank[:], queries, fp8_operand(k_q[b], tile_cols(h, BANK)), b == 0, b == r_passes - 1)
                 gates = kept([P, BANK], F32, f"gates{h}{m}")
                 nc.scalar.activation(gates[:], bank[:], SIGMOID, scale=SCORE_SCALE)
                 nc.sync.dma_start(out_0[tile_cols(m), tile_cols(h, BANK)], gates[:])

@@ -19,259 +19,267 @@ P = 128
 PACK = 4
 PASS = P * PACK
 BANK = 512
-QUADS = 4
+BANKS = 8
 SCORE_SCALE = 0.03125
-ROWS = 32
-TAB_AT, WV4_AT, PLANE = 0, J, J + N
-LATE_BYTES = 4 * 13312
+K_PASSES = K // PASS
+R_PASSES = R // PASS
+J_HALVES = J // BANK
+ROWS = 16 * K_PASSES
+PLANE = J + N
+LATE_WORDS = (K * N + K * R + K * M) // P
+STRIP = 256
+
+
+def cols(i, width=P):
+    return slice(i * width, (i + 1) * width)
 
 
 def tile_list_kvt_dl_sig_kernel(
     tc, tab_words, tab_scales, x, wq_words, wq_scales, wk, wv4_words, wv4_scales, wvd, offs, out_0, out_1
 ):
     nc = tc.nc
-    k_passes = K // PASS
-    r_passes = R // PASS
-    j_halves = J // BANK
+    on_vector, on_scalar = nc.vector.tensor_copy, nc.scalar.copy
 
     with ExitStack() as ctx:
         keep = ctx.enter_context(tc.tile_pool(name="keep", bufs=1))
-        ring = ctx.enter_context(tc.tile_pool(name="ring", bufs=2))
         staged = ctx.enter_context(tc.tile_pool(name="staged", bufs=1))
-        psum = ctx.enter_context(tc.psum_pool(name="psum", bufs=8))
+        psum = ctx.enter_context(tc.psum_pool(name="psum", bufs=1))
 
         def kept(shape, dtype, name, tag=None):
             return keep.tile(shape, dtype, name=name, tag=tag or name, align_bytes=64)
 
-        offsets = keep.tile([P, J // 16], U16, name="offsets")
-        nc.sync.dma_start(offsets[:], offs)
+        opened = []
 
-        def compact_rows(scales):
+        def next_bank():
+            bank = psum.tile([P, BANK], F32, name=f"bank{len(opened) % BANKS}")
+            opened.append(bank)
+            return bank
+
+        def scale_rows_of(scales):
             return scales.rearrange("a q n -> q a n").bitcast(I32)
 
-        scale_rows = kept([P, T], U8, "scale_rows")
-        nc.sync.dma_start(scale_rows[0:ROWS, :].bitcast(I32), compact_rows(tab_scales))
-        compact = kept([ROWS, PLANE], U8, "compact")
-        nc.sync.dma_start(compact[:, WV4_AT : WV4_AT + N].bitcast(I32), compact_rows(wv4_scales))
-        wq_rows = kept([ROWS, R], U8, "wq_rows")
-        nc.sync.dma_start(wq_rows[:].bitcast(I32), compact_rows(wq_scales))
-        table = kept([P, T], I32, "table")
-        nc.sync.dma_start(table[:], tab_words[0].rearrange("p t b -> p (t b)").bitcast(I32))
-
-        wv4_codes = kept([P, k_passes, 2 * N], U8, "wv4_codes")
-        nc.sync.dma_start(wv4_codes[:].bitcast(I32), wv4_words.rearrange("a p n -> p a n").bitcast(I32))
-        wvd_raw0 = kept([P, 1024], F32, "wvd_raw0")[:]
-        nc.sync.dma_start(wvd_raw0, wvd[0 * PASS : 1 * PASS, :].rearrange("(p j) n -> p (j n)", j=PACK))
-        nc.vector.memset(scale_rows[32:64, :].bitcast(I32), 0)
-        nc.vector.memset(scale_rows[64:128, :].bitcast(I32), 0)
-        planes = kept([P, k_passes * PLANE], U8, "planes")
-        nc.vector.memset(planes[:].bitcast(I32), 0)
-        wq_planes = kept([P, k_passes * R], U8, "wq_planes")
-        nc.vector.memset(wq_planes[:].bitcast(I32), 0)
-
-        warm_in = kept([P, 1], F32, "warm_in")
-        warm_out = kept([P, 1], F32, "warm_out")
-        nc.gpsimd.memset(warm_in[:], 0.0)
-        nc.scalar.activation(warm_out[:], warm_in[:], SIGMOID, scale=SCORE_SCALE)
-
-        def place(target, rows):
-            for q in (0, 2, 1, 3):
+        def place(planes, rows):
+            for quad in (0, 2, 1, 3):
                 nc.sync.dma_start(
-                    target[32 * q : 32 * q + 4, :].bitcast(I32).rearrange("p (a n) -> p a n", a=k_passes),
-                    rows[8 * q : 8 * q + 8, :].bitcast(I32),
+                    planes[32 * quad : 32 * quad + 4, :].bitcast(I32).rearrange("p (a n) -> p a n", a=K_PASSES),
+                    rows[8 * quad : 8 * quad + 8, :].bitcast(I32),
                 )
-
-        picked_rows = staged.tile([P, J], U8, name="picked_rows", align_bytes=64, offset=LATE_BYTES - J // 2)
-        nc.vector.tensor_copy(picked_rows[:], scale_rows[:].indirect(offsets[:]))
-        nc.vector.tensor_copy(compact[:, TAB_AT : TAB_AT + J].bitcast(I32), picked_rows[0:ROWS, :].bitcast(I32))
-        place(planes, compact)
-        wq_compact = staged.tile([ROWS, R], U8, name="wq_compact", align_bytes=64, offset=LATE_BYTES)
-        nc.vector.tensor_copy(
-            wq_compact[:].bitcast(I32).rearrange("p (b t h) -> p b t h", t=PACK, h=32),
-            wq_rows[:].bitcast(I32).rearrange("p (b h t) -> p b t h", t=PACK, h=32),
-        )
-
-        def plane_cols(a, start, cols):
-            first = a * PLANE + start
-            return planes[:, first + cols.start : first + cols.stop]
-
-        late = staged.tile([P, 13312], F32, name="late", align_bytes=64, offset=0)
-        wvd_raw1 = late[:, 0 : 1024]
-        nc.sync.dma_start(wvd_raw1, wvd[1 * PASS : 2 * PASS, :].rearrange("(p j) n -> p (j n)", j=PACK))
-        wk_raw00 = late[:, 5120 : 7168]
-        nc.sync.dma_start(wk_raw00.rearrange("p (j r) -> p j r", j=PACK), wk[0 * PASS : 1 * PASS, 0 * PASS : 1 * PASS].rearrange("(p j) r -> p j r", j=PACK))
-        wk_raw01 = late[:, 7168 : 9216]
-        nc.sync.dma_start(wk_raw01.rearrange("p (j r) -> p j r", j=PACK), wk[1 * PASS : 2 * PASS, 0 * PASS : 1 * PASS].rearrange("(p j) r -> p j r", j=PACK))
-        x_raw0 = late[:, 1024 : 3072]
-        nc.sync.dma_start(x_raw0, x[0 * PASS : 1 * PASS, :].rearrange("(p j) m -> p (j m)", j=PACK))
-        wq_loaded = kept([P, k_passes * R // 2], I32, "wq_loaded", tag="wq_rows")
-        nc.sync.dma_start(
-            wq_loaded[:].rearrange("p (a n) -> p a n", a=k_passes), wq_words.rearrange("a p n -> p a n").bitcast(I32)
-        )
-        place(wq_planes, wq_compact)
-        x_raw1 = late[:, 3072 : 5120]
-        nc.sync.dma_start(x_raw1, x[1 * PASS : 2 * PASS, :].rearrange("(p j) m -> p (j m)", j=PACK))
-        wk_raw10 = late[:, 9216 : 11264]
-        nc.sync.dma_start(wk_raw10.rearrange("p (j r) -> p j r", j=PACK), wk[0 * PASS : 1 * PASS, 1 * PASS : 2 * PASS].rearrange("(p j) r -> p j r", j=PACK))
-        wk_raw11 = late[:, 11264 : 13312]
-        nc.sync.dma_start(wk_raw11.rearrange("p (j r) -> p j r", j=PACK), wk[1 * PASS : 2 * PASS, 1 * PASS : 2 * PASS].rearrange("(p j) r -> p j r", j=PACK))
-        x_raw = [x_raw0, x_raw1]
-        wvd_raw = [wvd_raw0, wvd_raw1]
-        wk_raw = {(0, 0): wk_raw00, (0, 1): wk_raw01, (1, 0): wk_raw10, (1, 1): wk_raw11}
-
-        def tab_operand(a, h, cols):
-            codes = tab_codes[h][:, a, 2 * cols.start : 2 * cols.stop].bitcast(FP4X4)
-            return codes, plane_cols(a, TAB_AT + h * BANK, cols)
 
         def mx_tiles(width, name, tag=None):
             return kept([P, width], U32, name + "_codes", tag=tag), kept([P, width], U8, name + "_plane")
 
-        def quantize(quantized, cols, rounded):
+        def quantize(quantized, part, rounded):
             codes, plane = quantized
-            nc.vector.quantize_mx(out=codes[:, cols].bitcast(FP8X4), scales=plane[:, cols], in_=rounded)
+            nc.vector.quantize_mx(out=codes[:, part].bitcast(FP8X4), scales=plane[:, part], in_=rounded)
 
-        def fp8_operand(quantized, cols):
+        def fp8_operand(quantized, part):
             codes, plane = quantized
-            return codes[:, cols].bitcast(FP8X4), plane[:, cols]
+            return codes[:, part].bitcast(FP8X4), plane[:, part]
 
         def mx(out, stationary, moving, start, stop):
             nc.tensor.matmul_mx(
-                out=out, lhsT=stationary[0], lhsT_scale=stationary[1], rhs=moving[0], rhs_scale=moving[1],
-                start=start, stop=stop,
+                out=out,
+                lhsT=stationary[0],
+                lhsT_scale=stationary[1],
+                rhs=moving[0],
+                rhs_scale=moving[1],
+                start=start,
+                stop=stop,
             )
 
-        def tile_cols(i, width=P):
-            return slice(i * width, (i + 1) * width)
+        offsets = keep.tile([P, J // 16], U16, name="offsets")
+        nc.sync.dma_start(offsets[:], offs)
+        tab_rows = kept([P, T], U8, "tab_rows")
+        nc.sync.dma_start(tab_rows[0:ROWS, :].bitcast(I32), scale_rows_of(tab_scales))
+        value_rows = kept([ROWS, PLANE], U8, "value_rows")
+        nc.sync.dma_start(value_rows[:, J:PLANE].bitcast(I32), scale_rows_of(wv4_scales))
+        wq_rows = kept([ROWS, R], U8, "wq_rows")
+        nc.sync.dma_start(wq_rows[:].bitcast(I32), scale_rows_of(wq_scales))
+        table = kept([P, T], I32, "table")
+        nc.sync.dma_start(table[:], tab_words[0].rearrange("p t b -> p (t b)").bitcast(I32))
+        wv4_codes = kept([P, K_PASSES, 2 * N], U8, "wv4_codes")
+        nc.sync.dma_start(wv4_codes[:].bitcast(I32), wv4_words.rearrange("a p n -> p a n").bitcast(I32))
 
-        def project(waves, copies):
-            banks = [[psum.tile([P, BANK], F32, name="bank") for c in range(BANK // P)] for wave in waves]
-            rounded = [ring.tile([P, PACK * BANK], BF16, name="projected", bufs=6, align_bytes=64) for wave in waves]
-            for a in range(k_passes):
-                for w, (stationary, moving) in enumerate(waves):
-                    for c, bank in enumerate(banks[w]):
-                        for t in range(PACK):
-                            first = a == 0 and t == 0
-                            last = a == k_passes - 1 and t == PACK - 1
-                            mx(bank[:, tile_cols(t)], stationary(a, t), moving(a, tile_cols(c)), first, last)
-                        if a == k_passes - 1:
-                            copies[c % len(copies)](
-                                rounded[w][:, tile_cols(c, BANK)].rearrange("p (n t) -> p n t", t=PACK),
-                                bank[:].rearrange("p (t n) -> p n t", t=PACK),
-                            )
+        nc.vector.memset(tab_rows[32:64, :].bitcast(I32), 0)
+        nc.vector.memset(tab_rows[64:128, :].bitcast(I32), 0)
+        zero = kept([P, 1], F32, "zero")
+        nc.gpsimd.memset(zero[:], 0.0)
+        value_planes = kept([P, K_PASSES * PLANE], U8, "value_planes")
+        nc.gpsimd.memset(value_planes[:].bitcast(I32), 0)
+        wq_planes = kept([P, K_PASSES * R], U8, "wq_planes")
+        nc.gpsimd.memset(wq_planes[:].bitcast(I32), 0)
+        warm = kept([P, 1], F32, "warm")
+        nc.scalar.activation(warm[:], zero[:], SIGMOID, scale=SCORE_SCALE)
+
+        picked_rows = staged.tile([P, J], U8, name="picked_rows", align_bytes=64, offset=4 * LATE_WORDS - J // 2)
+        nc.vector.tensor_copy(picked_rows[:], tab_rows[:].indirect(offsets[:]))
+        nc.vector.tensor_copy(value_rows[:, 0:J].bitcast(I32), picked_rows[0:ROWS, :].bitcast(I32))
+        place(value_planes, value_rows)
+        wq_rows_sorted = staged.tile([ROWS, R], U8, name="wq_rows_sorted", align_bytes=64, offset=4 * LATE_WORDS)
+        nc.vector.tensor_copy(
+            wq_rows_sorted[:].bitcast(I32).rearrange("p (b t h) -> p b t h", t=PACK, h=32),
+            wq_rows[:].bitcast(I32).rearrange("p (b h t) -> p b t h", t=PACK, h=32),
+        )
+
+        late = staged.tile([P, LATE_WORDS], F32, name="late", align_bytes=64, offset=0)
+        taken = []
+
+        def load_pass(matrix, a, part):
+            width = part.stop - part.start
+            first = sum(taken)
+            taken.append(PACK * width)
+            raw = late[:, first : first + PACK * width]
+            nc.sync.dma_start(
+                raw.rearrange("p (j n) -> p j n", j=PACK),
+                matrix[cols(a, PASS), part].rearrange("(p j) n -> p j n", j=PACK),
+            )
+            return raw
+
+        wvd_raw = [load_pass(wvd, a, slice(0, N)) for a in range(K_PASSES)]
+        wk_raw = {(a, 0): load_pass(wk, a, cols(0, PASS)) for a in range(K_PASSES)}
+        x_raw = [load_pass(x, 0, slice(0, M))]
+        wq_loaded = kept([P, K_PASSES * R // 2], I32, "wq_loaded", tag="wq_rows")
+        nc.sync.dma_start(
+            wq_loaded[:].rearrange("p (a n) -> p a n", a=K_PASSES), wq_words.rearrange("a p n -> p a n").bitcast(I32)
+        )
+        place(wq_planes, wq_rows_sorted)
+        x_raw.append(load_pass(x, 1, slice(0, M)))
+        for a in range(K_PASSES):
+            wk_raw[a, 1] = load_pass(wk, a, cols(1, PASS))
+
+        tab_codes = {}
+        for h in range(J_HALVES):
+            picked = kept([P, BANK], U32, f"picked{h}", tag="picked")
+            nc.vector.tensor_copy(picked[:], table[:].bitcast(U32).indirect(offsets[:, cols(h, BANK // 16)]))
+            pairs = picked[:].bitcast(U16).rearrange("p (j d) -> p d j", d=K_PASSES)
+            for a in range(K_PASSES):
+                tab_codes[a, h] = kept([P, 2 * BANK], U8, f"tab_codes{a}{h}")[:]
+                nc.vector.tensor_copy(tab_codes[a, h].bitcast(U16), pairs[:, a, :])
+
+        def tab_operand(a, h, part):
+            first = a * PLANE + h * BANK
+            codes = tab_codes[a, h][:, 2 * part.start : 2 * part.stop].bitcast(FP4X4)
+            return codes, value_planes[:, first + part.start : first + part.stop]
+
+        def prepare(raw, width, name, copies, sort):
+            rounded = kept([P, PACK * width], BF16, name + "_rounded")
+            if sort:
+                dst = rounded[:].rearrange("p (t h i j) -> p t h j i", t=PACK, i=4, j=PACK)
+                src = raw.rearrange("p (j h t i) -> p t h j i", t=PACK, i=4, j=PACK)
+            else:
+                dst = rounded[:].rearrange("p (c i j) -> p c j i", i=4, j=PACK)
+                src = raw.rearrange("p (j c i) -> p c j i", i=4, j=PACK)
+            quantized = mx_tiles(width, name)
+            parts = len(copies)
+            for i, copy in enumerate(copies):
+                share = cols(i, dst.shape[1] // parts)
+                copy(dst[:, share], src[:, share])
+            for i in range(parts):
+                quantize(quantized, cols(i, width // parts), rounded[:, cols(i, PACK * width // parts)])
+            return quantized
+
+        def project(stationary, moving, copies, name):
+            banks = [next_bank() for copy in copies]
+            rounded = kept([P, len(copies) * BANK], BF16, name + "_projected")
+            for a in range(K_PASSES):
+                for c, bank in enumerate(banks):
+                    for t in range(PACK):
+                        first = a == 0 and t == 0
+                        last = a == K_PASSES - 1 and t == PACK - 1
+                        mx(bank[:, cols(t)], stationary(a, t), moving(a, c), first, last)
+                    if a == K_PASSES - 1:
+                        copies[c](
+                            rounded[:, cols(c, BANK)].rearrange("p (n t) -> p n t", t=PACK),
+                            bank[:].rearrange("p (t n) -> p n t", t=PACK),
+                        )
             return rounded
 
-        def wq_operand(b):
-            def operand(a, t):
-                col = PACK * b + t
-                codes = wq_codes[:, tile_cols(PACK * r_passes * a + col, 2 * P)].bitcast(FP4X4)
-                return codes, wq_planes[:, tile_cols(PACK * r_passes * a + col)]
-
-            return operand
-
-        tab_codes = []
-        for h in range(j_halves):
-            picked = kept([P, BANK], U32, f"picked{h}", tag="picked")
-            nc.vector.tensor_copy(picked[:], table[:].bitcast(U32).indirect(offsets[:, 32 * h : 32 * (h + 1)]))
-            parted = kept([P, k_passes, 2 * BANK], U8, f"tab_codes{h}")
-            nc.vector.tensor_copy(
-                parted[:].bitcast(U16), picked[:].bitcast(U16).rearrange("p (j d) -> p d j", d=k_passes)
-            )
-            tab_codes.append(parted)
-
-        wvd_q = []
-        for a in range(k_passes):
-            rounded = ring.tile([P, PACK * N], BF16, name="wvd_rounded", align_bytes=64)
-            [nc.scalar.copy, nc.scalar.copy][a](
-                rounded[:].rearrange("p (c i j) -> p c j i", i=4, j=PACK),
-                wvd_raw[a].rearrange("p (j c i) -> p c j i", i=4, j=PACK),
-            )
-            wvd_q.append(mx_tiles(N, f"wvd{a}"))
-            quantize(wvd_q[a], slice(0, N), rounded[:])
-
-        wk_q = {}
-
-        def prepare_wk(b):
-            for a in range(k_passes):
-                rounded = kept([P, PACK * BANK], BF16, f"wk_rounded{b}{a}")
-                dst = rounded[:].rearrange("p (t h i j) -> p t h j i", t=PACK, i=4, j=PACK)
-                src = wk_raw[b, a].rearrange("p (j h t i) -> p t h j i", t=PACK, i=4, j=PACK)
-                wk_q[a, b] = mx_tiles(PASS, f"wk{b}{a}")
-                for half in range(2):
-                    copy = [nc.vector.tensor_copy, nc.scalar.copy, nc.vector.tensor_copy, nc.vector.tensor_copy, nc.vector.tensor_copy, nc.vector.tensor_copy, nc.vector.tensor_copy, nc.vector.tensor_copy][4 * b + 2 * a + half]
-                    copy(dst[:, tile_cols(half, 2)], src[:, tile_cols(half, 2)])
-                for half in range(2):
-                    quantize(wk_q[a, b], tile_cols(half, PASS // 2), rounded[:, tile_cols(half, PACK * PASS // 2)])
-
-        def keys(b, h):
-            wave = (lambda a, t: fp8_operand(wk_q[a, b], tile_cols(t)), lambda a, cols: tab_operand(a, h, cols))
-            return project([wave], [[nc.scalar.copy], [nc.scalar.copy], [nc.scalar.copy, nc.scalar.copy, nc.scalar.copy, nc.vector.tensor_copy], [nc.scalar.copy, nc.vector.tensor_copy]][2 * b + h])[0]
-
-        prepare_wk(0)
         whole = slice(0, BANK)
+        wvd_q = [prepare(wvd_raw[a], N, f"wvd{a}", [on_scalar], False) for a in range(K_PASSES)]
+        wk_q = {(a, 0): prepare(wk_raw[a, 0], PASS, f"wk{a}0", [[on_vector, on_vector], [on_vector, on_vector]][a], True) for a in range(K_PASSES)}
+
         v_banks = {}
-        for h in range(j_halves):
+        for h in range(J_HALVES):
             for n in range(N // P):
-                v_banks[h, n] = psum.tile([P, BANK], F32, name="bank")
-                for a in range(k_passes):
-                    base = (
-                        wv4_codes[:, a, tile_cols(n, 2 * P)].bitcast(FP4X4),
-                        plane_cols(a, WV4_AT, tile_cols(n)),
-                    )
+                v_banks[h, n] = next_bank()
+            for a in range(K_PASSES):
+                for n in range(N // P):
+                    plane = value_planes[:, a * PLANE + J + n * P : a * PLANE + J + (n + 1) * P]
+                    base = (wv4_codes[:, a, cols(n, 2 * P)].bitcast(FP4X4), plane)
                     mx(v_banks[h, n][:], base, tab_operand(a, h, whole), a == 0, False)
         values = [kept([P, J], F32, f"values{n}") for n in range(N // P)]
-        for a in range(k_passes):
+        for a in range(K_PASSES):
             for n in range(N // P):
-                for h in range(j_halves):
-                    last = a == k_passes - 1
-                    mx(v_banks[h, n][:], fp8_operand(wvd_q[a], tile_cols(n)), tab_operand(a, h, whole), False, last)
+                for h in range(J_HALVES):
+                    last = a == K_PASSES - 1
+                    mx(v_banks[h, n][:], fp8_operand(wvd_q[a], cols(n)), tab_operand(a, h, whole), False, last)
                     if last:
-                        [nc.scalar.copy, nc.scalar.copy, nc.scalar.copy, nc.scalar.copy][2 * n + h](values[n][:, tile_cols(h, BANK)], v_banks[h, n][:])
+                        on_scalar(values[n][:, cols(h, BANK)], v_banks[h, n][:])
 
-        x_q = []
-        for a in range(k_passes):
-            rounded = kept([P, PACK * BANK], BF16, f"x_rounded{a}")
-            dst = rounded[:].rearrange("p (c i j) -> p c j i", i=4, j=PACK)
-            src = x_raw[a].rearrange("p (j c i) -> p c j i", i=4, j=PACK)
-            x_q.append(mx_tiles(M, f"x{a}"))
-            for half, copy in enumerate([[nc.vector.tensor_copy, nc.vector.tensor_copy], [nc.vector.tensor_copy, nc.vector.tensor_copy]][a]):
-                copy(dst[:, tile_cols(half, M // 8)], src[:, tile_cols(half, M // 8)])
-            for half in range(2):
-                quantize(x_q[a], tile_cols(half, M // 2), rounded[:, tile_cols(half, PACK * M // 2)])
-
-        wq_codes = kept([P, k_passes * 2 * R], U8, "wq_codes")
+        x_q = [prepare(x_raw[a], M, f"x{a}", [on_vector, on_vector], False) for a in range(K_PASSES)]
+        wq_codes = kept([P, K_PASSES * 2 * R], U8, "wq_codes")
         nc.vector.tensor_copy(
             wq_codes[:].bitcast(I32).rearrange("p (g t h w) -> p g t h w", t=PACK, h=32, w=2),
             wq_loaded[:].rearrange("p (g h t w) -> p g t h w", t=PACK, h=32, w=2),
         )
 
-        k_rounded = [keys(0, h) for h in range(j_halves)]
-        q_rounded = []
-        for b in range(r_passes):
-            wave = (wq_operand(b), lambda a, cols: fp8_operand(x_q[a], cols))
-            q_rounded.extend(project([wave], [[nc.scalar.copy], [nc.scalar.copy]][b]))
+        def keys(b, first_tile, copies, name):
+            def moving(a, c):
+                h, within = divmod(first_tile + c, BANK // P)
+                return tab_operand(a, h, cols(within))
 
-        prepare_wk(1)
-        k_q = [mx_tiles(J, "kr0", tag="x_rounded0"), mx_tiles(J, "kr1")]
-        for h in range(j_halves):
-            quantize(k_q[0], tile_cols(h, BANK), k_rounded[h][:])
-        q_q = mx_tiles(r_passes * M, "qr", tag="wk_rounded11")
-        for b in range(r_passes):
-            quantize(q_q, tile_cols(b, M), q_rounded[b][:])
+            return project(lambda a, t: fp8_operand(wk_q[a, b], cols(t)), moving, copies, name)
 
-        for h in range(j_halves):
-            rounded = keys(1, h)
-            for part in range(2):
-                quantize(k_q[1], tile_cols(2 * h + part, BANK // 2), rounded[:, tile_cols(part, PACK * BANK // 2)])
+        def queries(b):
+            def stationary(a, t):
+                col = PACK * (R_PASSES * a + b) + t
+                return wq_codes[:, cols(col, 2 * P)].bitcast(FP4X4), wq_planes[:, cols(col)]
+
+            return project(stationary, lambda a, c: fp8_operand(x_q[a], cols(c)), [on_scalar, on_scalar, on_scalar, on_scalar], f"qr{b}")
+
+        k_rounded = [keys(0, 4 * h, [on_scalar, on_scalar, on_scalar, on_scalar], f"kr0{h}") for h in range(J_HALVES)]
+        q_rounded = [queries(b) for b in range(R_PASSES)]
+        for a in range(K_PASSES):
+            wk_q[a, 1] = prepare(wk_raw[a, 1], PASS, f"wk{a}1", [on_vector, on_vector], True)
+
+        k_first = [mx_tiles(BANK, f"kr0{h}", tag=["x0_rounded","x1_rounded"][h]) for h in range(J_HALVES)]
+        for h in range(J_HALVES):
+            quantize(k_first[h], whole, k_rounded[h][:])
+        q_q = [mx_tiles(M, f"qr{b}", tag=["wk11_rounded",None][b]) for b in range(R_PASSES)]
+        for b in range(R_PASSES):
+            quantize(q_q[b], whole, q_rounded[b][:])
 
         for n in range(N // P):
-            nc.sync.dma_start(out_1[tile_cols(n), :], values[n][:])
+            nc.sync.dma_start(out_1[cols(n), :], values[n][:])
 
-        for h in range(j_halves):
-            for m in range(M // P):
-                bank = psum.tile([P, BANK], F32, name="bank")
-                for b in range(r_passes):
-                    queries = fp8_operand(q_q, tile_cols(b * (M // P) + m))
-                    mx(bank[:], queries, fp8_operand(k_q[b], tile_cols(h, BANK)), b == 0, b == r_passes - 1)
-                gates = kept([P, BANK], F32, f"gates{h}{m}")
+        strips = J // STRIP
+        k_second = []
+
+        def last_keys(s):
+            rounded = keys(1, s * (STRIP // P), [[on_scalar, on_scalar],[on_scalar, on_vector],[on_scalar, on_vector],[on_vector, on_vector]][s], f"kr1{s}")
+            k_second.append(mx_tiles(STRIP, f"kr1{s}"))
+            for part in range(STRIP // 256):
+                quantize(k_second[s], cols(part, 256), rounded[:, cols(part, 1024)])
+
+        def scores(s):
+            h, within = divmod(s, BANK // STRIP)
+            side = BANK // STRIP
+            for group in range(M // P // side):
+                bank = next_bank()
+                for i in range(side):
+                    m = group * side + i
+                    strip_keys = (fp8_operand(k_first[h], cols(within, STRIP)), fp8_operand(k_second[s], slice(0, STRIP)))
+                    for b in range(R_PASSES):
+                        mx(bank[:, cols(i, STRIP)], fp8_operand(q_q[b], cols(m)), strip_keys[b], b == 0, b == R_PASSES - 1)
+                gates = kept([P, BANK], F32, f"gates{s}{group}")
                 nc.scalar.activation(gates[:], bank[:], SIGMOID, scale=SCORE_SCALE)
-                nc.sync.dma_start(out_0[tile_cols(m), tile_cols(h, BANK)], gates[:])
+                nc.sync.dma_start(
+                    out_0[cols(group, side * P), cols(s, STRIP)].rearrange("(i p) n -> p i n", i=side),
+                    gates[:].rearrange("p (i n) -> p i n", i=side),
+                )
+
+        for s in range(strips + 2):
+            if s < strips:
+                last_keys(s)
+            if s >= 2:
+                scores(s - 2)

from contextlib import ExitStack

import concourse.mybir as mybir

K, R, M, N, T, J = 1024, 1024, 512, 256, 4096, 1024
FLOPS = 2 * (K * R * M + K * R * J + R * M * J + 2 * K * N * J)

F32 = mybir.dt.float32
BF16 = mybir.dt.bfloat16
I32 = mybir.dt.int32
U32 = mybir.dt.uint32
U16 = mybir.dt.uint16
U8 = mybir.dt.uint8
FP8X4 = mybir.dt.float8_e4m3fn_x4
FP4X4 = mybir.dt.float4_e2m1fn_x4
SIGMOID = mybir.ActivationFunctionType.Sigmoid

P = 128
PACK = 4
PASS = P * PACK
BANK = 512
BANKS = 8
SCORE_SCALE = 0.03125
K_PASSES = K // PASS
R_PASSES = R // PASS
J_HALVES = J // BANK
ROWS = 16 * K_PASSES
PLANE = J + N
LATE_WORDS = (K * N + K * R + K * M) // P
STRIP = 256


def cols(i, width=P):
    return slice(i * width, (i + 1) * width)


def tile_list_kvt_dl_sig_kernel(
    tc, tab_words, tab_scales, x, wq_words, wq_scales, wk, wv4_words, wv4_scales, wvd, offs, out_0, out_1
):
    nc = tc.nc
    on_vector, on_scalar = nc.vector.tensor_copy, nc.scalar.copy

    with ExitStack() as ctx:
        keep = ctx.enter_context(tc.tile_pool(name="keep", bufs=1))
        staged = ctx.enter_context(tc.tile_pool(name="staged", bufs=1))
        psum = ctx.enter_context(tc.psum_pool(name="psum", bufs=1))

        def kept(shape, dtype, name, tag=None):
            return keep.tile(shape, dtype, name=name, tag=tag or name, align_bytes=64)

        opened = []

        def next_bank():
            bank = psum.tile([P, BANK], F32, name=f"bank{len(opened) % BANKS}")
            opened.append(bank)
            return bank

        def scale_rows_of(scales):
            return scales.rearrange("a q n -> q a n").bitcast(I32)

        def place(planes, rows):
            for quad in (0, 2, 1, 3):
                nc.sync.dma_start(
                    planes[32 * quad : 32 * quad + 4, :].bitcast(I32).rearrange("p (a n) -> p a n", a=K_PASSES),
                    rows[8 * quad : 8 * quad + 8, :].bitcast(I32),
                )

        def mx_tiles(width, name, tag=None):
            return kept([P, width], U32, name + "_codes", tag=tag), kept([P, width], U8, name + "_plane")

        def quantize(quantized, part, rounded):
            codes, plane = quantized
            nc.vector.quantize_mx(out=codes[:, part].bitcast(FP8X4), scales=plane[:, part], in_=rounded)

        def fp8_operand(quantized, part):
            codes, plane = quantized
            return codes[:, part].bitcast(FP8X4), plane[:, part]

        def mx(out, stationary, moving, start, stop):
            nc.tensor.matmul_mx(
                out=out,
                lhsT=stationary[0],
                lhsT_scale=stationary[1],
                rhs=moving[0],
                rhs_scale=moving[1],
                start=start,
                stop=stop,
            )

        offsets = keep.tile([P, J // 16], U16, name="offsets")
        nc.sync.dma_start(offsets[:], offs)
        tab_rows = kept([P, T], U8, "tab_rows")
        nc.sync.dma_start(tab_rows[0:ROWS, :].bitcast(I32), scale_rows_of(tab_scales))
        value_rows = kept([ROWS, PLANE], U8, "value_rows")
        nc.sync.dma_start(value_rows[:, J:PLANE].bitcast(I32), scale_rows_of(wv4_scales))
        wq_rows = kept([ROWS, R], U8, "wq_rows")
        nc.sync.dma_start(wq_rows[:].bitcast(I32), scale_rows_of(wq_scales))
        table = kept([P, T], I32, "table")
        nc.sync.dma_start(table[:], tab_words[0].rearrange("p t b -> p (t b)").bitcast(I32))
        wv4_codes = kept([P, K_PASSES, 2 * N], U8, "wv4_codes")
        nc.sync.dma_start(wv4_codes[:].bitcast(I32), wv4_words.rearrange("a p n -> p a n").bitcast(I32))

        nc.vector.memset(tab_rows[32:64, :].bitcast(I32), 0)
        nc.vector.memset(tab_rows[64:128, :].bitcast(I32), 0)
        zero = kept([P, 1], F32, "zero")
        nc.gpsimd.memset(zero[:], 0.0)
        value_planes = kept([P, K_PASSES * PLANE], U8, "value_planes")
        nc.gpsimd.memset(value_planes[:].bitcast(I32), 0)
        wq_planes = kept([P, K_PASSES * R], U8, "wq_planes")
        nc.gpsimd.memset(wq_planes[:].bitcast(I32), 0)
        warm = kept([P, 1], F32, "warm")
        nc.scalar.activation(warm[:], zero[:], SIGMOID, scale=SCORE_SCALE)

        picked_rows = staged.tile([P, J], U8, name="picked_rows", align_bytes=64, offset=4 * LATE_WORDS - J // 2)
        nc.vector.tensor_copy(picked_rows[:], tab_rows[:].indirect(offsets[:]))
        nc.vector.tensor_copy(value_rows[:, 0:J].bitcast(I32), picked_rows[0:ROWS, :].bitcast(I32))
        place(value_planes, value_rows)
        wq_rows_sorted = staged.tile([ROWS, R], U8, name="wq_rows_sorted", align_bytes=64, offset=4 * LATE_WORDS)
        nc.vector.tensor_copy(
            wq_rows_sorted[:].bitcast(I32).rearrange("p (b t h) -> p b t h", t=PACK, h=32),
            wq_rows[:].bitcast(I32).rearrange("p (b h t) -> p b t h", t=PACK, h=32),
        )

        late = staged.tile([P, LATE_WORDS], F32, name="late", align_bytes=64, offset=0)
        taken = []

        def load_pass(matrix, a, part):
            width = part.stop - part.start
            first = sum(taken)
            taken.append(PACK * width)
            raw = late[:, first : first + PACK * width]
            nc.sync.dma_start(
                raw.rearrange("p (j n) -> p j n", j=PACK),
                matrix[cols(a, PASS), part].rearrange("(p j) n -> p j n", j=PACK),
            )
            return raw

        wvd_raw = [load_pass(wvd, a, slice(0, N)) for a in range(K_PASSES)]
        wk_raw = {(a, 0): load_pass(wk, a, cols(0, PASS)) for a in range(K_PASSES)}
        x_raw = [load_pass(x, 0, slice(0, M))]
        wq_loaded = kept([P, K_PASSES * R // 2], I32, "wq_loaded", tag="wq_rows")
        nc.sync.dma_start(
            wq_loaded[:].rearrange("p (a n) -> p a n", a=K_PASSES), wq_words.rearrange("a p n -> p a n").bitcast(I32)
        )
        place(wq_planes, wq_rows_sorted)
        x_raw.append(load_pass(x, 1, slice(0, M)))
        for a in range(K_PASSES):
            wk_raw[a, 1] = load_pass(wk, a, cols(1, PASS))

        tab_codes = {}
        for h in range(J_HALVES):
            picked = kept([P, BANK], U32, f"picked{h}", tag="picked")
            nc.vector.tensor_copy(picked[:], table[:].bitcast(U32).indirect(offsets[:, cols(h, BANK // 16)]))
            pairs = picked[:].bitcast(U16).rearrange("p (j d) -> p d j", d=K_PASSES)
            for a in range(K_PASSES):
                tab_codes[a, h] = kept([P, 2 * BANK], U8, f"tab_codes{a}{h}")[:]
                nc.vector.tensor_copy(tab_codes[a, h].bitcast(U16), pairs[:, a, :])

        def tab_operand(a, h, part):
            first = a * PLANE + h * BANK
            codes = tab_codes[a, h][:, 2 * part.start : 2 * part.stop].bitcast(FP4X4)
            return codes, value_planes[:, first + part.start : first + part.stop]

        def prepare(raw, width, name, copies, sort):
            rounded = kept([P, PACK * width], BF16, name + "_rounded")
            if sort:
                dst = rounded[:].rearrange("p (t h i j) -> p t h j i", t=PACK, i=4, j=PACK)
                src = raw.rearrange("p (j h t i) -> p t h j i", t=PACK, i=4, j=PACK)
            else:
                dst = rounded[:].rearrange("p (c i j) -> p c j i", i=4, j=PACK)
                src = raw.rearrange("p (j c i) -> p c j i", i=4, j=PACK)
            quantized = mx_tiles(width, name)
            parts = len(copies)
            for i, copy in enumerate(copies):
                share = cols(i, dst.shape[1] // parts)
                copy(dst[:, share], src[:, share])
            for i in range(parts):
                quantize(quantized, cols(i, width // parts), rounded[:, cols(i, PACK * width // parts)])
            return quantized

        def project(stationary, moving, copies, name):
            banks = [next_bank() for copy in copies]
            rounded = kept([P, len(copies) * BANK], BF16, name + "_projected")
            for a in range(K_PASSES):
                for c, bank in enumerate(banks):
                    for t in range(PACK):
                        first = a == 0 and t == 0
                        last = a == K_PASSES - 1 and t == PACK - 1
                        mx(bank[:, cols(t)], stationary(a, t), moving(a, c), first, last)
                    if a == K_PASSES - 1:
                        copies[c](
                            rounded[:, cols(c, BANK)].rearrange("p (n t) -> p n t", t=PACK),
                            bank[:].rearrange("p (t n) -> p n t", t=PACK),
                        )
            return rounded

        whole = slice(0, BANK)
        wvd_q = [prepare(wvd_raw[a], N, f"wvd{a}", [on_scalar], False) for a in range(K_PASSES)]
        wk_q = {(a, 0): prepare(wk_raw[a, 0], PASS, f"wk{a}0", [[on_vector, on_vector], [on_vector, on_vector]][a], True) for a in range(K_PASSES)}

        v_banks = {}
        for h in range(J_HALVES):
            for n in range(N // P):
                v_banks[h, n] = next_bank()
            for a in range(K_PASSES):
                for n in range(N // P):
                    plane = value_planes[:, a * PLANE + J + n * P : a * PLANE + J + (n + 1) * P]
                    base = (wv4_codes[:, a, cols(n, 2 * P)].bitcast(FP4X4), plane)
                    mx(v_banks[h, n][:], base, tab_operand(a, h, whole), a == 0, False)
        values = [kept([P, J], F32, f"values{n}") for n in range(N // P)]
        for a in range(K_PASSES):
            for n in range(N // P):
                for h in range(J_HALVES):
                    last = a == K_PASSES - 1
                    mx(v_banks[h, n][:], fp8_operand(wvd_q[a], cols(n)), tab_operand(a, h, whole), False, last)
                    if last:
                        on_scalar(values[n][:, cols(h, BANK)], v_banks[h, n][:])

        x_q = [prepare(x_raw[a], M, f"x{a}", [on_vector, on_vector], False) for a in range(K_PASSES)]
        wq_codes = kept([P, K_PASSES * 2 * R], U8, "wq_codes")
        nc.vector.tensor_copy(
            wq_codes[:].bitcast(I32).rearrange("p (g t h w) -> p g t h w", t=PACK, h=32, w=2),
            wq_loaded[:].rearrange("p (g h t w) -> p g t h w", t=PACK, h=32, w=2),
        )

        def keys(b, first_tile, copies, name):
            def moving(a, c):
                h, within = divmod(first_tile + c, BANK // P)
                return tab_operand(a, h, cols(within))

            return project(lambda a, t: fp8_operand(wk_q[a, b], cols(t)), moving, copies, name)

        def queries(b):
            def stationary(a, t):
                col = PACK * (R_PASSES * a + b) + t
                return wq_codes[:, cols(col, 2 * P)].bitcast(FP4X4), wq_planes[:, cols(col)]

            return project(stationary, lambda a, c: fp8_operand(x_q[a], cols(c)), [on_scalar, on_scalar, on_scalar, on_scalar], f"qr{b}")

        k_rounded = [keys(0, 4 * h, [on_scalar, on_scalar, on_scalar, on_scalar], f"kr0{h}") for h in range(J_HALVES)]
        q_rounded = [queries(b) for b in range(R_PASSES)]
        for a in range(K_PASSES):
            wk_q[a, 1] = prepare(wk_raw[a, 1], PASS, f"wk{a}1", [on_vector, on_vector], True)

        k_first = [mx_tiles(BANK, f"kr0{h}", tag=["x0_rounded","x1_rounded"][h]) for h in range(J_HALVES)]
        for h in range(J_HALVES):
            quantize(k_first[h], whole, k_rounded[h][:])
        q_q = [mx_tiles(M, f"qr{b}", tag=["wk11_rounded",None][b]) for b in range(R_PASSES)]
        for b in range(R_PASSES):
            quantize(q_q[b], whole, q_rounded[b][:])

        for n in range(N // P):
            nc.sync.dma_start(out_1[cols(n), :], values[n][:])

        strips = J // STRIP
        k_second = []

        def last_keys(s):
            rounded = keys(1, s * (STRIP // P), [[on_scalar, on_scalar],[on_scalar, on_vector],[on_scalar, on_vector],[on_vector, on_vector]][s], f"kr1{s}")
            k_second.append(mx_tiles(STRIP, f"kr1{s}"))
            for part in range(STRIP // 256):
                quantize(k_second[s], cols(part, 256), rounded[:, cols(part, 1024)])

        def scores(s):
            h, within = divmod(s, BANK // STRIP)
            side = BANK // STRIP
            for group in range(M // P // side):
                bank = next_bank()
                for i in range(side):
                    m = group * side + i
                    strip_keys = (fp8_operand(k_first[h], cols(within, STRIP)), fp8_operand(k_second[s], slice(0, STRIP)))
                    for b in range(R_PASSES):
                        mx(bank[:, cols(i, STRIP)], fp8_operand(q_q[b], cols(m)), strip_keys[b], b == 0, b == R_PASSES - 1)
                gates = kept([P, BANK], F32, f"gates{s}{group}")
                nc.scalar.activation(gates[:], bank[:], SIGMOID, scale=SCORE_SCALE)
                nc.sync.dma_start(
                    out_0[cols(group, side * P), cols(s, STRIP)].rearrange("(i p) n -> p i n", i=side),
                    gates[:].rearrange("p (i n) -> p i n", i=side),
                )

        for s in range(strips + 2):
            if s < strips:
                last_keys(s)
            if s >= 2:
                scores(s - 2)
